import numpy as np
import ml_dtypes

BF16 = ml_dtypes.bfloat16


def bf(x):
    return np.asarray(x, np.float32).astype(BF16)


def f32(x):
    return np.asarray(x, np.float32)


def f64(x):
    return np.asarray(x).astype(np.float64)


def striped(idx):
    return np.tile(idx.reshape(-1, 16).T, (8, 1))


S, K, M, N, D, V = 1024, 256, 512, 1024, 16, 64


def gelu_tanh(v):
    return 0.5 * v * (1.0 + np.tanh(np.sqrt(2.0 / np.pi) * (v + 0.044715 * v**3)))


def setup_inputs():
    return {"table": bf(np.random.standard_normal((K, S))), "w": bf(np.random.standard_normal((K, M)) / np.sqrt(K)), "b": f32(0.5 * np.random.standard_normal((M, 1))), "offs": striped(np.random.permutation(np.tile(np.arange(S), 2))[:N])}


def reference(table, w, b, offs):
    idx = offs[:16].T.reshape(-1)
    x = f64(table)[:, idx]
    y = f64(w).T @ x
    z = gelu_tanh(y + f64(b))
    return z.reshape(M, V, D).max(axis=2)

@@ -1,0 +1,56 @@
+import concourse.mybir as mybir
+
+BF16, F32, U16 = mybir.dt.bfloat16, mybir.dt.float32, mybir.dt.uint16
+GELU = mybir.ActivationFunctionType.Gelu_apprx_tanh
+
+P = 128
+K, S = 256, 1024
+M, N = 512, 1024
+NEIGHBOURS = 16
+PIECE = 512
+K_BLOCKS, M_BLOCKS, PIECES = K // P, M // P, N // PIECE
+OFFSET_COLUMNS = PIECE // 16
+POOLED = PIECE // NEIGHBOURS
+
+FLOPS = 2 * K * M * N
+
+
+def tile_gather_matmul_kernel(tc, table, w, b, offs, out):
+    nc = tc.nc
+    with (
+        tc.tile_pool(name="held", bufs=1) as held,
+        tc.tile_pool(name="work", bufs=3) as work,
+        tc.psum_pool(name="psum", bufs=4) as psum,
+    ):
+        offsets = held.tile([P, N // 16], U16, name="offsets")
+        nc.sync.dma_start(offsets[:], offs)
+        windows = [held.tile([P, S], BF16, name=f"window{kb}") for kb in range(K_BLOCKS)]
+        weights = [held.tile([P, M], BF16, name=f"weights{kb}") for kb in range(K_BLOCKS)]
+        for kb in range(K_BLOCKS):
+            nc.sync.dma_start(windows[kb][:], table[kb * P : (kb + 1) * P, :])
+            nc.scalar.dma_start(weights[kb][:], w[kb * P : (kb + 1) * P, :])
+        bias = held.tile([P, M_BLOCKS], F32, name="bias")
+        nc.gpsimd.dma_start(bias[:], b.rearrange("(mb p) o -> p (mb o)", p=P))
+
+        for mb in range(M_BLOCKS):
+            pooled = work.tile([P, PIECES * POOLED], F32, name="pooled")
+            for piece in range(PIECES):
+                picked = offsets[:, piece * OFFSET_COLUMNS : (piece + 1) * OFFSET_COLUMNS]
+                bank = psum.tile([P, PIECE], F32, name="bank")
+                for kb in range(K_BLOCKS):
+                    nc.tensor.matmul(
+                        bank[:],
+                        weights[kb][:, mb * P : (mb + 1) * P],
+                        windows[kb][:].indirect(picked),
+                        start=(kb == 0),
+                        stop=(kb == K_BLOCKS - 1),
+                    )
+                z = work.tile([P, PIECE], F32, name="z")
+                nc.scalar.activation(z[:], bank[:], GELU, bias=bias[:, mb : mb + 1])
+                nc.vector.tensor_reduce(
+                    pooled[:, piece * POOLED : (piece + 1) * POOLED],
+                    z[:].rearrange("p (v t) -> p v t", t=NEIGHBOURS),
+                    axis=mybir.AxisListType.X,
+                    op=mybir.AluOpType.max,
+                )
+            nc.sync.dma_start(out[mb * P : (mb + 1) * P, :], pooled[:])

@@ -11,6 +11,7 @@ PIECE = 512
 K_BLOCKS, M_BLOCKS, PIECES = K // P, M // P, N // PIECE
 OFFSET_COLUMNS = PIECE // 16
 POOLED = PIECE // NEIGHBOURS
+WARM_UP_MATMULS = 6
 
 FLOPS = 2 * K * M * N
 
@@ -20,33 +21,45 @@ def tile_gather_matmul_kernel(tc, table, w, b, offs, out):
     with (
         tc.tile_pool(name="held", bufs=1) as held,
         tc.tile_pool(name="work", bufs=3) as work,
-        tc.psum_pool(name="psum", bufs=4) as psum,
+        tc.psum_pool(name="psum", bufs=3) as psum,
+        tc.psum_pool(name="unread", bufs=1) as unread,
     ):
         offsets = held.tile([P, N // 16], U16, name="offsets")
         nc.sync.dma_start(offsets[:], offs)
         windows = [held.tile([P, S], BF16, name=f"window{kb}") for kb in range(K_BLOCKS)]
         weights = [held.tile([P, M], BF16, name=f"weights{kb}") for kb in range(K_BLOCKS)]
         for kb in range(K_BLOCKS):
-            nc.sync.dma_start(windows[kb][:], table[kb * P : (kb + 1) * P, :])
-            nc.scalar.dma_start(weights[kb][:], w[kb * P : (kb + 1) * P, :])
+            nc.scalar.dma_start(windows[kb][:], table[kb * P : (kb + 1) * P, :])
+            nc.sync.dma_start(weights[kb][:], w[kb * P : (kb + 1) * P, :])
         bias = held.tile([P, M_BLOCKS], F32, name="bias")
-        nc.gpsimd.dma_start(bias[:], b.rearrange("(mb p) o -> p (mb o)", p=P))
+        nc.sync.dma_start(bias[:], b.rearrange("(mb p) o -> p (mb o)", p=P))
 
+        zeros = held.tile([P, PIECE], BF16, name="zeros")
+        nc.vector.memset(zeros[:], 0.0)
+        unread_bank = unread.tile([P, PIECE], F32, name="unread_bank")
+        for turn in range(WARM_UP_MATMULS):
+            nc.tensor.matmul(unread_bank[:], zeros[:, 0:P], zeros[:], start=True, stop=True)
+        unread_gelu = held.tile([P, 1], F32, name="unread_gelu")
+        nc.scalar.activation(unread_gelu[:], zeros[:, 0:1], GELU)
+
+        picked = [
+            offsets[:, piece * OFFSET_COLUMNS : (piece + 1) * OFFSET_COLUMNS] for piece in range(PIECES)
+        ]
         for mb in range(M_BLOCKS):
             pooled = work.tile([P, PIECES * POOLED], F32, name="pooled")
-            for piece in range(PIECES):
-                picked = offsets[:, piece * OFFSET_COLUMNS : (piece + 1) * OFFSET_COLUMNS]
-                bank = psum.tile([P, PIECE], F32, name="bank")
-                for kb in range(K_BLOCKS):
+            banks = [psum.tile([P, PIECE], F32, name=f"bank{piece}") for piece in range(PIECES)]
+            for kb in range(K_BLOCKS):
+                for piece in range(PIECES):
                     nc.tensor.matmul(
-                        bank[:],
+                        banks[piece][:],
                         weights[kb][:, mb * P : (mb + 1) * P],
-                        windows[kb][:].indirect(picked),
+                        windows[kb][:].indirect(picked[piece]),
                         start=(kb == 0),
                         stop=(kb == K_BLOCKS - 1),
                     )
+            for piece in range(PIECES):
                 z = work.tile([P, PIECE], F32, name="z")
-                nc.scalar.activation(z[:], bank[:], GELU, bias=bias[:, mb : mb + 1])
+                nc.scalar.activation(z[:], banks[piece][:], GELU, bias=bias[:, mb : mb + 1])
                 nc.vector.tensor_reduce(
                     pooled[:, piece * POOLED : (piece + 1) * POOLED],
                     z[:].rearrange("p (v t) -> p v t", t=NEIGHBOURS),

@@ -10,8 +10,7 @@ NEIGHBOURS = 16
 PIECE = 512
 K_BLOCKS, M_BLOCKS, PIECES = K // P, M // P, N // PIECE
 OFFSET_COLUMNS = PIECE // 16
-POOLED = PIECE // NEIGHBOURS
-WARM_UP_MATMULS = 6
+HALF = PIECE // 2
 
 FLOPS = 2 * K * M * N
 
@@ -21,49 +20,41 @@ def tile_gather_matmul_kernel(tc, table, w, b, offs, out):
     with (
         tc.tile_pool(name="held", bufs=1) as held,
         tc.tile_pool(name="work", bufs=3) as work,
-        tc.psum_pool(name="psum", bufs=3) as psum,
-        tc.psum_pool(name="unread", bufs=1) as unread,
+        tc.psum_pool(name="psum", bufs=4) as psum,
     ):
         offsets = held.tile([P, N // 16], U16, name="offsets")
         nc.sync.dma_start(offsets[:], offs)
         windows = [held.tile([P, S], BF16, name=f"window{kb}") for kb in range(K_BLOCKS)]
         weights = [held.tile([P, M], BF16, name=f"weights{kb}") for kb in range(K_BLOCKS)]
         for kb in range(K_BLOCKS):
-            nc.scalar.dma_start(windows[kb][:], table[kb * P : (kb + 1) * P, :])
-            nc.sync.dma_start(weights[kb][:], w[kb * P : (kb + 1) * P, :])
+            nc.sync.dma_start(windows[kb][:], table[kb * P : (kb + 1) * P, :])
+            nc.scalar.dma_start(weights[kb][:], w[kb * P : (kb + 1) * P, :])
         bias = held.tile([P, M_BLOCKS], F32, name="bias")
-        nc.sync.dma_start(bias[:], b.rearrange("(mb p) o -> p (mb o)", p=P))
+        nc.gpsimd.dma_start(bias[:], b.rearrange("(mb p) o -> p (mb o)", p=P))
 
-        zeros = held.tile([P, PIECE], BF16, name="zeros")
-        nc.vector.memset(zeros[:], 0.0)
-        unread_bank = unread.tile([P, PIECE], F32, name="unread_bank")
-        for turn in range(WARM_UP_MATMULS):
-            nc.tensor.matmul(unread_bank[:], zeros[:, 0:P], zeros[:], start=True, stop=True)
-        unread_gelu = held.tile([P, 1], F32, name="unread_gelu")
-        nc.scalar.activation(unread_gelu[:], zeros[:, 0:1], GELU)
-
-        picked = [
-            offsets[:, piece * OFFSET_COLUMNS : (piece + 1) * OFFSET_COLUMNS] for piece in range(PIECES)
-        ]
         for mb in range(M_BLOCKS):
-            pooled = work.tile([P, PIECES * POOLED], F32, name="pooled")
-            banks = [psum.tile([P, PIECE], F32, name=f"bank{piece}") for piece in range(PIECES)]
-            for kb in range(K_BLOCKS):
-                for piece in range(PIECES):
+            pooled = work.tile([P, N // NEIGHBOURS], F32, name="pooled")
+            for piece in range(PIECES):
+                picked = offsets[:, piece * OFFSET_COLUMNS : (piece + 1) * OFFSET_COLUMNS]
+                bank = psum.tile([P, PIECE], F32, name="bank")
+                for kb in range(K_BLOCKS):
                     nc.tensor.matmul(
-                        banks[piece][:],
+                        bank[:],
                         weights[kb][:, mb * P : (mb + 1) * P],
-                        windows[kb][:].indirect(picked[piece]),
+                        windows[kb][:].indirect(picked),
                         start=(kb == 0),
                         stop=(kb == K_BLOCKS - 1),
                     )
-            for piece in range(PIECES):
-                z = work.tile([P, PIECE], F32, name="z")
-                nc.scalar.activation(z[:], banks[piece][:], GELU, bias=bias[:, mb : mb + 1])
-                nc.vector.tensor_reduce(
-                    pooled[:, piece * POOLED : (piece + 1) * POOLED],
-                    z[:].rearrange("p (v t) -> p v t", t=NEIGHBOURS),
-                    axis=mybir.AxisListType.X,
-                    op=mybir.AluOpType.max,
-                )
+                for half in range(2):
+                    z = work.tile([P, HALF], F32, name="z")
+                    nc.scalar.activation(
+                        z[:], bank[:, half * HALF : (half + 1) * HALF], GELU, bias=bias[:, mb : mb + 1]
+                    )
+                    first = (piece * PIECE + half * HALF) // NEIGHBOURS
+                    nc.vector.tensor_reduce(
+                        pooled[:, first : first + HALF // NEIGHBOURS],
+                        z[:].rearrange("p (v t) -> p v t", t=NEIGHBOURS),
+                        axis=mybir.AxisListType.X,
+                        op=mybir.AluOpType.max,
+                    )
             nc.sync.dma_start(out[mb * P : (mb + 1) * P, :], pooled[:])

@@ -11,6 +11,7 @@ PIECE = 512
 K_BLOCKS, M_BLOCKS, PIECES = K // P, M // P, N // PIECE
 OFFSET_COLUMNS = PIECE // 16
 HALF = PIECE // 2
+WARM_UP_MATMULS = 3
 
 FLOPS = 2 * K * M * N
 
@@ -21,6 +22,7 @@ def tile_gather_matmul_kernel(tc, table, w, b, offs, out):
         tc.tile_pool(name="held", bufs=1) as held,
         tc.tile_pool(name="work", bufs=3) as work,
         tc.psum_pool(name="psum", bufs=4) as psum,
+        tc.psum_pool(name="unread", bufs=1) as unread,
     ):
         offsets = held.tile([P, N // 16], U16, name="offsets")
         nc.sync.dma_start(offsets[:], offs)
@@ -31,6 +33,12 @@ def tile_gather_matmul_kernel(tc, table, w, b, offs, out):
             nc.scalar.dma_start(weights[kb][:], w[kb * P : (kb + 1) * P, :])
         bias = held.tile([P, M_BLOCKS], F32, name="bias")
         nc.gpsimd.dma_start(bias[:], b.rearrange("(mb p) o -> p (mb o)", p=P))
+
+        zeros = held.tile([P, PIECE], BF16, name="zeros")
+        nc.vector.memset(zeros[:], 0.0)
+        unread_bank = unread.tile([P, PIECE], F32, name="unread_bank")
+        for turn in range(WARM_UP_MATMULS):
+            nc.tensor.matmul(unread_bank[:], zeros[:, 0:P], zeros[:], start=True, stop=True)
 
         for mb in range(M_BLOCKS):
             pooled = work.tile([P, N // NEIGHBOURS], F32, name="pooled")

@@ -11,7 +11,6 @@ PIECE = 512
 K_BLOCKS, M_BLOCKS, PIECES = K // P, M // P, N // PIECE
 OFFSET_COLUMNS = PIECE // 16
 HALF = PIECE // 2
-WARM_UP_MATMULS = 3
 
 FLOPS = 2 * K * M * N
 
@@ -22,41 +21,44 @@ def tile_gather_matmul_kernel(tc, table, w, b, offs, out):
         tc.tile_pool(name="held", bufs=1) as held,
         tc.tile_pool(name="work", bufs=3) as work,
         tc.psum_pool(name="psum", bufs=4) as psum,
-        tc.psum_pool(name="unread", bufs=1) as unread,
     ):
         offsets = held.tile([P, N // 16], U16, name="offsets")
         nc.sync.dma_start(offsets[:], offs)
         windows = [held.tile([P, S], BF16, name=f"window{kb}") for kb in range(K_BLOCKS)]
         weights = [held.tile([P, M], BF16, name=f"weights{kb}") for kb in range(K_BLOCKS)]
         for kb in range(K_BLOCKS):
-            nc.sync.dma_start(windows[kb][:], table[kb * P : (kb + 1) * P, :])
-            nc.scalar.dma_start(weights[kb][:], w[kb * P : (kb + 1) * P, :])
+            nc.scalar.dma_start(windows[kb][:], table[kb * P : (kb + 1) * P, :])
+            nc.sync.dma_start(weights[kb][:], w[kb * P : (kb + 1) * P, :])
         bias = held.tile([P, M_BLOCKS], F32, name="bias")
-        nc.gpsimd.dma_start(bias[:], b.rearrange("(mb p) o -> p (mb o)", p=P))
+        nc.sync.dma_start(bias[:], b.rearrange("(mb p) o -> p (mb o)", p=P))
 
-        zeros = held.tile([P, PIECE], BF16, name="zeros")
-        nc.vector.memset(zeros[:], 0.0)
-        unread_bank = unread.tile([P, PIECE], F32, name="unread_bank")
-        for turn in range(WARM_UP_MATMULS):
-            nc.tensor.matmul(unread_bank[:], zeros[:, 0:P], zeros[:], start=True, stop=True)
+        unread = held.tile([P, 1], F32, name="unread")
+        nc.vector.memset(unread[:], 0.0)
+        nc.scalar.activation(unread[:], unread[:], GELU)
 
+        picked = [
+            offsets[:, piece * OFFSET_COLUMNS : (piece + 1) * OFFSET_COLUMNS] for piece in range(PIECES)
+        ]
         for mb in range(M_BLOCKS):
             pooled = work.tile([P, N // NEIGHBOURS], F32, name="pooled")
-            for piece in range(PIECES):
-                picked = offsets[:, piece * OFFSET_COLUMNS : (piece + 1) * OFFSET_COLUMNS]
-                bank = psum.tile([P, PIECE], F32, name="bank")
-                for kb in range(K_BLOCKS):
+            banks = [psum.tile([P, PIECE], F32, name=f"bank{piece}") for piece in range(PIECES)]
+            for kb in range(K_BLOCKS):
+                for piece in range(PIECES):
                     nc.tensor.matmul(
-                        bank[:],
+                        banks[piece][:],
                         weights[kb][:, mb * P : (mb + 1) * P],
-                        windows[kb][:].indirect(picked),
+                        windows[kb][:].indirect(picked[piece]),
                         start=(kb == 0),
                         stop=(kb == K_BLOCKS - 1),
                     )
+            for piece in range(PIECES):
                 for half in range(2):
                     z = work.tile([P, HALF], F32, name="z")
                     nc.scalar.activation(
-                        z[:], bank[:, half * HALF : (half + 1) * HALF], GELU, bias=bias[:, mb : mb + 1]
+                        z[:],
+                        banks[piece][:, half * HALF : (half + 1) * HALF],
+                        GELU,
+                        bias=bias[:, mb : mb + 1],
                     )
                     first = (piece * PIECE + half * HALF) // NEIGHBOURS
                     nc.vector.tensor_reduce(

@@ -42,15 +42,18 @@ def tile_gather_matmul_kernel(tc, table, w, b, offs, out):
         for mb in range(M_BLOCKS):
             pooled = work.tile([P, N // NEIGHBOURS], F32, name="pooled")
             banks = [psum.tile([P, PIECE], F32, name=f"bank{piece}") for piece in range(PIECES)]
-            for kb in range(K_BLOCKS):
-                for piece in range(PIECES):
-                    nc.tensor.matmul(
-                        banks[piece][:],
-                        weights[kb][:, mb * P : (mb + 1) * P],
-                        windows[kb][:].indirect(picked[piece]),
-                        start=(kb == 0),
-                        stop=(kb == K_BLOCKS - 1),
-                    )
+            if mb == 0:
+                order = [(kb, piece) for kb in range(K_BLOCKS) for piece in range(PIECES)]
+            else:
+                order = [(kb, piece) for piece in range(PIECES) for kb in range(K_BLOCKS)]
+            for kb, piece in order:
+                nc.tensor.matmul(
+                    banks[piece][:],
+                    weights[kb][:, mb * P : (mb + 1) * P],
+                    windows[kb][:].indirect(picked[piece]),
+                    start=(kb == 0),
+                    stop=(kb == K_BLOCKS - 1),
+                )
             for piece in range(PIECES):
                 for half in range(2):
                     z = work.tile([P, HALF], F32, name="z")

@@ -23,13 +23,14 @@ def tile_gather_matmul_kernel(tc, table, w, b, offs, out):
         tc.psum_pool(name="psum", bufs=4) as psum,
     ):
         offsets = held.tile([P, N // 16], U16, name="offsets")
-        nc.sync.dma_start(offsets[:], offs)
         windows = [held.tile([P, S], BF16, name=f"window{kb}") for kb in range(K_BLOCKS)]
         weights = [held.tile([P, M], BF16, name=f"weights{kb}") for kb in range(K_BLOCKS)]
-        for kb in range(K_BLOCKS):
-            nc.scalar.dma_start(windows[kb][:], table[kb * P : (kb + 1) * P, :])
-            nc.sync.dma_start(weights[kb][:], w[kb * P : (kb + 1) * P, :])
         bias = held.tile([P, M_BLOCKS], F32, name="bias")
+        nc.sync.dma_start(windows[0][:], table[0:P, :])
+        nc.scalar.dma_start(weights[0][:], w[0:P, :])
+        nc.sync.dma_start(offsets[:], offs)
+        nc.sync.dma_start(windows[1][:], table[P : 2 * P, :])
+        nc.scalar.dma_start(weights[1][:], w[P : 2 * P, :])
         nc.sync.dma_start(bias[:], b.rearrange("(mb p) o -> p (mb o)", p=P))
 
         unread = held.tile([P, 1], F32, name="unread")

@@ -10,7 +10,7 @@ NEIGHBOURS = 16
 PIECE = 512
 K_BLOCKS, M_BLOCKS, PIECES = K // P, M // P, N // PIECE
 OFFSET_COLUMNS = PIECE // 16
-HALF = PIECE // 2
+HALF = PIECE // 4
 
 FLOPS = 2 * K * M * N
 
@@ -19,7 +19,7 @@ def tile_gather_matmul_kernel(tc, table, w, b, offs, out):
     nc = tc.nc
     with (
         tc.tile_pool(name="held", bufs=1) as held,
-        tc.tile_pool(name="work", bufs=3) as work,
+        tc.tile_pool(name="work", bufs=8) as work,
         tc.psum_pool(name="psum", bufs=4) as psum,
     ):
         offsets = held.tile([P, N // 16], U16, name="offsets")
@@ -56,7 +56,7 @@ def tile_gather_matmul_kernel(tc, table, w, b, offs, out):
                     stop=(kb == K_BLOCKS - 1),
                 )
             for piece in range(PIECES):
-                for half in range(2):
+                for half in range(PIECE // HALF):
                     z = work.tile([P, HALF], F32, name="z")
                     nc.scalar.activation(
                         z[:],

@@ -10,7 +10,7 @@ NEIGHBOURS = 16
 PIECE = 512
 K_BLOCKS, M_BLOCKS, PIECES = K // P, M // P, N // PIECE
 OFFSET_COLUMNS = PIECE // 16
-HALF = PIECE // 4
+STEP = PIECE // 4
 
 FLOPS = 2 * K * M * N
 
@@ -24,14 +24,21 @@ def tile_gather_matmul_kernel(tc, table, w, b, offs, out):
     ):
         offsets = held.tile([P, N // 16], U16, name="offsets")
         windows = [held.tile([P, S], BF16, name=f"window{kb}") for kb in range(K_BLOCKS)]
-        weights = [held.tile([P, M], BF16, name=f"weights{kb}") for kb in range(K_BLOCKS)]
+        weights_first = held.tile([P, K_BLOCKS, P], BF16, name="weights_first")
+        weights_rest = held.tile([P, K_BLOCKS, M - P], BF16, name="weights_rest")
+        w_by_block = w.rearrange("(kb p) m -> p kb m", p=P)
         bias = held.tile([P, M_BLOCKS], F32, name="bias")
         nc.sync.dma_start(windows[0][:], table[0:P, :])
-        nc.scalar.dma_start(weights[0][:], w[0:P, :])
+        nc.scalar.dma_start(weights_first[:], w_by_block[:, :, 0:P])
         nc.sync.dma_start(offsets[:], offs)
         nc.sync.dma_start(windows[1][:], table[P : 2 * P, :])
-        nc.scalar.dma_start(weights[1][:], w[P : 2 * P, :])
+        nc.scalar.dma_start(weights_rest[:], w_by_block[:, :, P:M])
         nc.sync.dma_start(bias[:], b.rearrange("(mb p) o -> p (mb o)", p=P))
+
+        def weights(kb, mb):
+            if mb == 0:
+                return weights_first[:, kb, :]
+            return weights_rest[:, kb, (mb - 1) * P : mb * P]
 
         unread = held.tile([P, 1], F32, name="unread")
         nc.vector.memset(unread[:], 0.0)
@@ -50,23 +57,23 @@ def tile_gather_matmul_kernel(tc, table, w, b, offs, out):
             for kb, piece in order:
                 nc.tensor.matmul(
                     banks[piece][:],
-                    weights[kb][:, mb * P : (mb + 1) * P],
+                    weights(kb, mb),
                     windows[kb][:].indirect(picked[piece]),
                     start=(kb == 0),
                     stop=(kb == K_BLOCKS - 1),
                 )
             for piece in range(PIECES):
-                for half in range(PIECE // HALF):
-                    z = work.tile([P, HALF], F32, name="z")
+                for step in range(PIECE // STEP):
+                    z = work.tile([P, STEP], F32, name="z")
                     nc.scalar.activation(
                         z[:],
-                        banks[piece][:, half * HALF : (half + 1) * HALF],
+                        banks[piece][:, step * STEP : (step + 1) * STEP],
                         GELU,
                         bias=bias[:, mb : mb + 1],
                     )
-                    first = (piece * PIECE + half * HALF) // NEIGHBOURS
+                    first = (piece * PIECE + step * STEP) // NEIGHBOURS
                     nc.vector.tensor_reduce(
-                        pooled[:, first : first + HALF // NEIGHBOURS],
+                        pooled[:, first : first + STEP // NEIGHBOURS],
                         z[:].rearrange("p (v t) -> p v t", t=NEIGHBOURS),
                         axis=mybir.AxisListType.X,
                         op=mybir.AluOpType.max,

@@ -40,10 +40,6 @@ def tile_gather_matmul_kernel(tc, table, w, b, offs, out):
                 return weights_first[:, kb, :]
             return weights_rest[:, kb, (mb - 1) * P : mb * P]
 
-        unread = held.tile([P, 1], F32, name="unread")
-        nc.vector.memset(unread[:], 0.0)
-        nc.scalar.activation(unread[:], unread[:], GELU)
-
         picked = [
             offsets[:, piece * OFFSET_COLUMNS : (piece + 1) * OFFSET_COLUMNS] for piece in range(PIECES)
         ]

@@ -10,7 +10,7 @@ NEIGHBOURS = 16
 PIECE = 512
 K_BLOCKS, M_BLOCKS, PIECES = K // P, M // P, N // PIECE
 OFFSET_COLUMNS = PIECE // 16
-STEP = PIECE // 4
+STEP = PIECE // 8
 
 FLOPS = 2 * K * M * N
 
@@ -44,7 +44,6 @@ def tile_gather_matmul_kernel(tc, table, w, b, offs, out):
             offsets[:, piece * OFFSET_COLUMNS : (piece + 1) * OFFSET_COLUMNS] for piece in range(PIECES)
         ]
         for mb in range(M_BLOCKS):
-            pooled = work.tile([P, N // NEIGHBOURS], F32, name="pooled")
             banks = [psum.tile([P, PIECE], F32, name=f"bank{piece}") for piece in range(PIECES)]
             if mb == 0:
                 order = [(kb, piece) for kb in range(K_BLOCKS) for piece in range(PIECES)]
@@ -59,6 +58,7 @@ def tile_gather_matmul_kernel(tc, table, w, b, offs, out):
                     stop=(kb == K_BLOCKS - 1),
                 )
             for piece in range(PIECES):
+                pooled = work.tile([P, PIECE // NEIGHBOURS], F32, name="pooled")
                 for step in range(PIECE // STEP):
                     z = work.tile([P, STEP], F32, name="z")
                     nc.scalar.activation(
@@ -67,11 +67,12 @@ def tile_gather_matmul_kernel(tc, table, w, b, offs, out):
                         GELU,
                         bias=bias[:, mb : mb + 1],
                     )
-                    first = (piece * PIECE + step * STEP) // NEIGHBOURS
+                    first = step * STEP // NEIGHBOURS
                     nc.vector.tensor_reduce(
                         pooled[:, first : first + STEP // NEIGHBOURS],
                         z[:].rearrange("p (v t) -> p v t", t=NEIGHBOURS),
                         axis=mybir.AxisListType.X,
                         op=mybir.AluOpType.max,
                     )
-            nc.sync.dma_start(out[mb * P : (mb + 1) * P, :], pooled[:])
+                nodes = PIECE // NEIGHBOURS
+                nc.sync.dma_start(out[mb * P : (mb + 1) * P, piece * nodes : (piece + 1) * nodes], pooled[:])

import concourse.mybir as mybir

BF16, F32, U16 = mybir.dt.bfloat16, mybir.dt.float32, mybir.dt.uint16
GELU = mybir.ActivationFunctionType.Gelu_apprx_tanh

P = 128
K, S = 256, 1024
M, N = 512, 1024
NEIGHBOURS = 16
PIECE = 512
K_BLOCKS, M_BLOCKS, PIECES = K // P, M // P, N // PIECE
OFFSET_COLUMNS = PIECE // 16
STEP = PIECE // 8

FLOPS = 2 * K * M * N


def tile_gather_matmul_kernel(tc, table, w, b, offs, out):
    nc = tc.nc
    with (
        tc.tile_pool(name="held", bufs=1) as held,
        tc.tile_pool(name="work", bufs=8) as work,
        tc.psum_pool(name="psum", bufs=4) as psum,
    ):
        offsets = held.tile([P, N // 16], U16, name="offsets")
        windows = [held.tile([P, S], BF16, name=f"window{kb}") for kb in range(K_BLOCKS)]
        weights_first = held.tile([P, K_BLOCKS, P], BF16, name="weights_first")
        weights_rest = held.tile([P, K_BLOCKS, M - P], BF16, name="weights_rest")
        w_by_block = w.rearrange("(kb p) m -> p kb m", p=P)
        bias = held.tile([P, M_BLOCKS], F32, name="bias")
        nc.sync.dma_start(windows[0][:], table[0:P, :])
        nc.scalar.dma_start(weights_first[:], w_by_block[:, :, 0:P])
        nc.sync.dma_start(offsets[:], offs)
        nc.sync.dma_start(windows[1][:], table[P : 2 * P, :])
        nc.scalar.dma_start(weights_rest[:], w_by_block[:, :, P:M])
        nc.sync.dma_start(bias[:], b.rearrange("(mb p) o -> p (mb o)", p=P))

        def weights(kb, mb):
            if mb == 0:
                return weights_first[:, kb, :]
            return weights_rest[:, kb, (mb - 1) * P : mb * P]

        picked = [
            offsets[:, piece * OFFSET_COLUMNS : (piece + 1) * OFFSET_COLUMNS] for piece in range(PIECES)
        ]
        for mb in range(M_BLOCKS):
            banks = [psum.tile([P, PIECE], F32, name=f"bank{piece}") for piece in range(PIECES)]
            if mb == 0:
                order = [(kb, piece) for kb in range(K_BLOCKS) for piece in range(PIECES)]
            else:
                order = [(kb, piece) for piece in range(PIECES) for kb in range(K_BLOCKS)]
            for kb, piece in order:
                nc.tensor.matmul(
                    banks[piece][:],
                    weights(kb, mb),
                    windows[kb][:].indirect(picked[piece]),
                    start=(kb == 0),
                    stop=(kb == K_BLOCKS - 1),
                )
            for piece in range(PIECES):
                pooled = work.tile([P, PIECE // NEIGHBOURS], F32, name="pooled")
                for step in range(PIECE // STEP):
                    z = work.tile([P, STEP], F32, name="z")
                    nc.scalar.activation(
                        z[:],
                        banks[piece][:, step * STEP : (step + 1) * STEP],
                        GELU,
                        bias=bias[:, mb : mb + 1],
                    )
                    first = step * STEP // NEIGHBOURS
                    nc.vector.tensor_reduce(
                        pooled[:, first : first + STEP // NEIGHBOURS],
                        z[:].rearrange("p (v t) -> p v t", t=NEIGHBOURS),
                        axis=mybir.AxisListType.X,
                        op=mybir.AluOpType.max,
                    )
                nodes = PIECE // NEIGHBOURS
                nc.sync.dma_start(out[mb * P : (mb + 1) * P, piece * nodes : (piece + 1) * nodes], pooled[:])
